import numpy as np, ml_dtypes
CORES = [24,25,26,27,28,29,30,31,224,225,226,227,228,229,230,231]
N = 16
F = 128
def setup_inputs(rng):
    return {"a": rng.standard_normal((N, 128, 128), dtype=np.float32).astype(ml_dtypes.bfloat16), "w": rng.standard_normal((N, 128, F), dtype=np.float32).astype(ml_dtypes.bfloat16)}
def setup_inputs_big(rng):
    d = setup_inputs(rng)
    for k in ("a", "w"): d[k] = (d[k].astype(np.float32) * 1024.0).astype(d[k].dtype)
    return d
def setup_inputs_small(rng):
    d = setup_inputs(rng)
    for k in ("a", "w"): d[k] = (d[k].astype(np.float32) * (1 / 1024.0)).astype(d[k].dtype)
    return d
def setup_inputs_apart(rng):
    d = setup_inputs(rng)
    f = (10.0 ** rng.permutation(np.linspace(-1.5, 1.5, N))).astype(np.float32).reshape(N, 1, 1)
    for k in ("a", "w"): d[k] = (d[k].astype(np.float32) * f).astype(d[k].dtype)
    return d
def setup_inputs_neg(rng):
    d = setup_inputs(rng)
    d["a"] = (np.abs(d["a"].astype(np.float32)) * 1048576.0).astype(d["a"].dtype); d["w"] = (-np.abs(d["w"].astype(np.float32))).astype(d["w"].dtype)
    return d
def reference(a, w):
    A, W = a.astype(np.float64), w.astype(np.float64)
    p = np.stack([A[j].T @ W[j] for j in range(N)])
    return {"y": np.maximum.accumulate(p, axis=0).astype(ml_dtypes.bfloat16)}

@@ -1,0 +1,101 @@
+from concourse.bass import DstId, RemoteDMATransfer
+from concourse.mybir import AluOpType
+
+F = 128
+PER = 8
+
+SCRATCH = {
+    "a_sb": ("sbuf", [128, 128], "bfloat16"),
+    "w_sb": ("sbuf", [128, F], "bfloat16"),
+    "slots": ("sbuf", [128, PER * F], "bfloat16"),
+    "low": ("sbuf", [128, F], "bfloat16"),
+    "out": ("sbuf", [128, F], "bfloat16"),
+    "acc": ("psum", [128, F], "float32"),
+}
+SEMAPHORES = ["ld", "mm", "vp", "vacc", "vout", "st", "sent", "lowarr"] + ["arr%d" % k for k in range(PER)]
+
+
+def _count(mask):
+    return bin(mask).count("1")
+
+
+def _write(g, topo, core, srcs, dst_cores, dst_ap, remote_sem, local_sem, alu_op):
+    mask = topo.mask(core, dst_cores[0])
+    for d in dst_cores:
+        mask &= topo.mask(core, d)
+    ids = []
+    for d in dst_cores:
+        rid, pid = topo.addr(d, core)
+        ids.append(DstId(rid=rid, pnc=pid))
+    g.remote_dma_fused([RemoteDMATransfer(dst_ids=ids, dma_engine_mask=mask, remote_sem=remote_sem, srcs=srcs,
+                                          dsts=[dst_ap for _ in dst_cores], alu_op=alu_op)], local_sem=local_sem)
+    return _count(mask)
+
+
+def rank_program(g, core, T, topo):
+    if T.rank_of(core) is None:
+        return
+    S = T.sem
+
+    def place(c):
+        return (topo.host(c), topo.chip(c))
+
+    lo_chip = [c for c in T.cores if place(c) == place(T.cores[0])]
+    hi_chip = [c for c in T.cores if place(c) != place(T.cores[0])]
+    mine = lo_chip if core in lo_chip else hi_chip
+    me = mine.index(core)
+    owners = [c for c in lo_chip if all(topo.may_write(c, d) for d in hi_chip)]
+
+    def block(k):
+        return T.slots[:, k * F:(k + 1) * F]
+
+    def share(owner):
+        peers = [c for c in owners if topo.die(c) == topo.die(owner)]
+        return [d for d in hi_chip if topo.die(d) == topo.die(owner)][peers.index(owner)::len(peers)]
+
+    g.sync.dma_start(T.a_sb[:], T.a[:]).then_inc(S.ld, 16)
+    g.scalar.dma_start(T.w_sb[:], T.w[:]).then_inc(S.ld, 16)
+    g.tensor.wait_ge(S.ld, 32)
+    g.tensor.matmul(T.acc[:], T.a_sb[:], T.w_sb[:], start=True, stop=True).then_inc(S.mm, 1)
+    g.vector.wait_ge(S.mm, 1)
+    g.vector.tensor_copy(block(me), T.acc[:]).then_inc(S.vp, 1)
+
+    later = mine[me + 1:]
+    urgent = [c for c in owners if c != core] if mine is lo_chip else []
+    rest = [c for c in later if c not in urgent]
+    sent = 0
+    g.wait_ge(S.vp, 1)
+    for group in (urgent, rest):
+        if group:
+            sent += _write(g, topo, core, [block(me)], group, block(me), S["arr%d" % me], S.sent, 0)
+
+    on_chip = _count(topo.mask(mine[0], mine[1]))
+    if core in owners:
+        for k in range(len(mine)):
+            if k != me:
+                g.wait_ge(S["arr%d" % k], on_chip)
+        sent += _write(g, topo, core, [block(k) for k in range(len(mine))], share(core), T.low[:], S.lowarr, S.sent, 2)
+    if sent:
+        g.wait_ge(S.sent, sent)
+
+    steps = [(S["arr%d" % k], on_chip, block(k)) for k in range(me - 1, -1, -1)]
+    if mine is hi_chip:
+        owner = [c for c in owners if core in share(c)][0]
+        steps.append((S.lowarr, _count(topo.mask(owner, core)), T.low[:]))
+    g.vector.wait_ge(S.vp, 1)
+    for i, (sem, n, ap) in enumerate(steps):
+        g.vector.wait_ge(sem, n)
+        if i:
+            g.vector.wait_ge(S.vacc, i)
+        if i == len(steps) - 1:
+            g.vector.tensor_tensor(T.out[:], T.acc[:], ap, AluOpType.max).then_inc(S.vout, 1)
+        else:
+            g.vector.tensor_tensor(T.acc[:], T.acc[:], ap, AluOpType.max).then_inc(S.vacc, 1)
+
+    if steps:
+        g.sync.wait_ge(S.vout, 1)
+        g.sync.dma_start(T.y[:], T.out[:]).then_inc(S.st, 16)
+    else:
+        g.sync.wait_ge(S.vp, 1)
+        g.sync.dma_start(T.y[:], block(me)).then_inc(S.st, 16)
+    g.sync.wait_ge(S.st, 16)

@@ -3,33 +3,23 @@ from concourse.mybir import AluOpType
 
 F = 128
 PER = 8
+NP = 4
+W = F // NP
 
 SCRATCH = {
     "a_sb": ("sbuf", [128, 128], "bfloat16"),
     "w_sb": ("sbuf", [128, F], "bfloat16"),
     "slots": ("sbuf", [128, PER * F], "bfloat16"),
+    "parts": ("sbuf", [128, PER * W], "bfloat16"),
     "low": ("sbuf", [128, F], "bfloat16"),
     "out": ("sbuf", [128, F], "bfloat16"),
     "acc": ("psum", [128, F], "float32"),
 }
-SEMAPHORES = ["ld", "mm", "vp", "vacc", "vout", "st", "sent", "lowarr"] + ["arr%d" % k for k in range(PER)]
+SEMAPHORES = ["ld", "mm", "vp", "vacc", "vout", "st", "sent", "parr", "fararr", "lowarr"] + ["arr%d" % k for k in range(PER)]
 
 
 def _count(mask):
     return bin(mask).count("1")
-
-
-def _write(g, topo, core, srcs, dst_cores, dst_ap, remote_sem, local_sem, alu_op):
-    mask = topo.mask(core, dst_cores[0])
-    for d in dst_cores:
-        mask &= topo.mask(core, d)
-    ids = []
-    for d in dst_cores:
-        rid, pid = topo.addr(d, core)
-        ids.append(DstId(rid=rid, pnc=pid))
-    g.remote_dma_fused([RemoteDMATransfer(dst_ids=ids, dma_engine_mask=mask, remote_sem=remote_sem, srcs=srcs,
-                                          dsts=[dst_ap for _ in dst_cores], alu_op=alu_op)], local_sem=local_sem)
-    return _count(mask)
 
 
 def rank_program(g, core, T, topo):
@@ -45,13 +35,34 @@ def rank_program(g, core, T, topo):
     mine = lo_chip if core in lo_chip else hi_chip
     me = mine.index(core)
     owners = [c for c in lo_chip if all(topo.may_write(c, d) for d in hi_chip)]
+    near = topo.mask(mine[0], mine[1])
+    far = topo.mask(owners[0], hi_chip[0])
+    bits = [1 << i for i in range(near.bit_length()) if near >> i & 1]
+    per = len(bits) // NP
+    groups = [sum(bits[i * per:(i + 1) * per]) for i in range(NP)]
+
+    def entry(owner):
+        peers = [c for c in owners if topo.die(c) == topo.die(owner)]
+        return [d for d in hi_chip if topo.die(d) == topo.die(owner)][peers.index(owner)]
+
+    entries = [entry(o) for o in owners]
 
     def block(k):
         return T.slots[:, k * F:(k + 1) * F]
 
-    def share(owner):
-        peers = [c for c in owners if topo.die(c) == topo.die(owner)]
-        return [d for d in hi_chip if topo.die(d) == topo.die(owner)][peers.index(owner)::len(peers)]
+    def transfer(srcs, dst_cores, dst_ap, sem, mask, alu_op):
+        ids = []
+        for d in dst_cores:
+            rid, pid = topo.addr(d, core)
+            ids.append(DstId(rid=rid, pnc=pid))
+        return RemoteDMATransfer(dst_ids=ids, dma_engine_mask=mask, remote_sem=sem, srcs=srcs,
+                                 dsts=[dst_ap for _ in dst_cores], alu_op=alu_op)
+
+    sent = [0]
+
+    def call(transfers, engines):
+        g.remote_dma_fused(transfers, local_sem=S.sent)
+        sent[0] += engines
 
     g.sync.dma_start(T.a_sb[:], T.a[:]).then_inc(S.ld, 16)
     g.scalar.dma_start(T.w_sb[:], T.w[:]).then_inc(S.ld, 16)
@@ -59,32 +70,44 @@ def rank_program(g, core, T, topo):
     g.tensor.matmul(T.acc[:], T.a_sb[:], T.w_sb[:], start=True, stop=True).then_inc(S.mm, 1)
     g.vector.wait_ge(S.mm, 1)
     g.vector.tensor_copy(block(me), T.acc[:]).then_inc(S.vp, 1)
+    g.wait_ge(S.vp, 1)
+
+    def piece(p):
+        return T.slots[:, me * F + p * W:me * F + (p + 1) * W]
+
+    if mine is lo_chip:
+        todo = [p for p in range(NP) if owners[p] != core]
+        call([transfer([piece(p)], [owners[p]], T.parts[:, me * W:(me + 1) * W], S.parr, groups[i], 0)
+              for i, p in enumerate(todo)], per * len(todo))
+        if core in owners:
+            p = owners.index(core)
+            g.wait_ge(S.parr, per * (len(mine) - 1))
+            srcs = [piece(p) if k == me else T.parts[:, k * W:(k + 1) * W] for k in range(len(mine))]
+            call([transfer(srcs, [entries[p]], T.low[:, p * W:(p + 1) * W], S.fararr, far, 2)], _count(far))
 
     later = mine[me + 1:]
-    urgent = [c for c in owners if c != core] if mine is lo_chip else []
-    rest = [c for c in later if c not in urgent]
-    sent = 0
-    g.wait_ge(S.vp, 1)
-    for group in (urgent, rest):
-        if group:
-            sent += _write(g, topo, core, [block(me)], group, block(me), S["arr%d" % me], S.sent, 0)
+    if later:
+        call([transfer([block(me)], later, block(me), S["arr%d" % me], near, 0)], _count(near))
 
-    on_chip = _count(topo.mask(mine[0], mine[1]))
-    if core in owners:
-        for k in range(len(mine)):
-            if k != me:
-                g.wait_ge(S["arr%d" % k], on_chip)
-        sent += _write(g, topo, core, [block(k) for k in range(len(mine))], share(core), T.low[:], S.lowarr, S.sent, 2)
-    if sent:
-        g.wait_ge(S.sent, sent)
+    if core in entries:
+        p = entries.index(core)
+        g.wait_ge(S.fararr, _count(far))
+        call([transfer([T.low[:, p * W:(p + 1) * W]], [c for c in mine if c != core], T.low[:, p * W:(p + 1) * W], S.lowarr,
+                       near, 0)], _count(near))
+    if sent[0]:
+        g.wait_ge(S.sent, sent[0])
 
-    steps = [(S["arr%d" % k], on_chip, block(k)) for k in range(me - 1, -1, -1)]
+    before = [k for k in range(me - 1, -1, -1) if mine[k] not in owners] + [k for k in range(me - 1, -1, -1) if mine[k] in owners]
+    steps = [([(S["arr%d" % k], _count(near))], block(k)) for k in before]
     if mine is hi_chip:
-        owner = [c for c in owners if core in share(c)][0]
-        steps.append((S.lowarr, _count(topo.mask(owner, core)), T.low[:]))
+        waits = [(S.lowarr, _count(near) * len([c for c in entries if c != core]))]
+        if core in entries:
+            waits.append((S.fararr, _count(far)))
+        steps.append((waits, T.low[:]))
     g.vector.wait_ge(S.vp, 1)
-    for i, (sem, n, ap) in enumerate(steps):
-        g.vector.wait_ge(sem, n)
+    for i, (waits, ap) in enumerate(steps):
+        for sem, n in waits:
+            g.vector.wait_ge(sem, n)
         if i:
             g.vector.wait_ge(S.vacc, i)
         if i == len(steps) - 1:

from concourse.bass import DstId, RemoteDMATransfer
from concourse.mybir import AluOpType

F = 128
PER = 8
NP = 4
W = F // NP

SCRATCH = {
    "a_sb": ("sbuf", [128, 128], "bfloat16"),
    "w_sb": ("sbuf", [128, F], "bfloat16"),
    "slots": ("sbuf", [128, PER * F], "bfloat16"),
    "parts": ("sbuf", [128, PER * W], "bfloat16"),
    "low": ("sbuf", [128, F], "bfloat16"),
    "out": ("sbuf", [128, F], "bfloat16"),
    "acc": ("psum", [128, F], "float32"),
}
SEMAPHORES = ["ld", "mm", "vp", "vacc", "vout", "st", "sent", "parr", "fararr", "lowarr"] + ["arr%d" % k for k in range(PER)]


def _count(mask):
    return bin(mask).count("1")


def rank_program(g, core, T, topo):
    if T.rank_of(core) is None:
        return
    S = T.sem

    def place(c):
        return (topo.host(c), topo.chip(c))

    lo_chip = [c for c in T.cores if place(c) == place(T.cores[0])]
    hi_chip = [c for c in T.cores if place(c) != place(T.cores[0])]
    mine = lo_chip if core in lo_chip else hi_chip
    me = mine.index(core)
    owners = [c for c in lo_chip if all(topo.may_write(c, d) for d in hi_chip)]
    near = topo.mask(mine[0], mine[1])
    far = topo.mask(owners[0], hi_chip[0])
    bits = [1 << i for i in range(near.bit_length()) if near >> i & 1]
    per = len(bits) // NP
    groups = [sum(bits[i * per:(i + 1) * per]) for i in range(NP)]

    def entry(owner):
        peers = [c for c in owners if topo.die(c) == topo.die(owner)]
        return [d for d in hi_chip if topo.die(d) == topo.die(owner)][peers.index(owner)]

    entries = [entry(o) for o in owners]

    def block(k):
        return T.slots[:, k * F:(k + 1) * F]

    def transfer(srcs, dst_cores, dst_ap, sem, mask, alu_op):
        ids = []
        for d in dst_cores:
            rid, pid = topo.addr(d, core)
            ids.append(DstId(rid=rid, pnc=pid))
        return RemoteDMATransfer(dst_ids=ids, dma_engine_mask=mask, remote_sem=sem, srcs=srcs,
                                 dsts=[dst_ap for _ in dst_cores], alu_op=alu_op)

    sent = [0]

    def call(transfers, engines):
        g.remote_dma_fused(transfers, local_sem=S.sent)
        sent[0] += engines

    g.sync.dma_start(T.a_sb[:], T.a[:]).then_inc(S.ld, 16)
    g.scalar.dma_start(T.w_sb[:], T.w[:]).then_inc(S.ld, 16)
    g.tensor.wait_ge(S.ld, 32)
    g.tensor.matmul(T.acc[:], T.a_sb[:], T.w_sb[:], start=True, stop=True).then_inc(S.mm, 1)
    g.vector.wait_ge(S.mm, 1)
    g.vector.tensor_copy(block(me), T.acc[:]).then_inc(S.vp, 1)
    g.wait_ge(S.vp, 1)

    def piece(p):
        return T.slots[:, me * F + p * W:me * F + (p + 1) * W]

    if mine is lo_chip:
        todo = [p for p in range(NP) if owners[p] != core]
        call([transfer([piece(p)], [owners[p]], T.parts[:, me * W:(me + 1) * W], S.parr, groups[i], 0)
              for i, p in enumerate(todo)], per * len(todo))
        if core in owners:
            p = owners.index(core)
            g.wait_ge(S.parr, per * (len(mine) - 1))
            srcs = [piece(p) if k == me else T.parts[:, k * W:(k + 1) * W] for k in range(len(mine))]
            call([transfer(srcs, [entries[p]], T.low[:, p * W:(p + 1) * W], S.fararr, far, 2)], _count(far))

    later = mine[me + 1:]
    if later:
        call([transfer([block(me)], later, block(me), S["arr%d" % me], near, 0)], _count(near))

    if core in entries:
        p = entries.index(core)
        g.wait_ge(S.fararr, _count(far))
        call([transfer([T.low[:, p * W:(p + 1) * W]], [c for c in mine if c != core], T.low[:, p * W:(p + 1) * W], S.lowarr,
                       near, 0)], _count(near))
    if sent[0]:
        g.wait_ge(S.sent, sent[0])

    before = [k for k in range(me - 1, -1, -1) if mine[k] not in owners] + [k for k in range(me - 1, -1, -1) if mine[k] in owners]
    steps = [([(S["arr%d" % k], _count(near))], block(k)) for k in before]
    if mine is hi_chip:
        waits = [(S.lowarr, _count(near) * len([c for c in entries if c != core]))]
        if core in entries:
            waits.append((S.fararr, _count(far)))
        steps.append((waits, T.low[:]))
    g.vector.wait_ge(S.vp, 1)
    for i, (waits, ap) in enumerate(steps):
        for sem, n in waits:
            g.vector.wait_ge(sem, n)
        if i:
            g.vector.wait_ge(S.vacc, i)
        if i == len(steps) - 1:
            g.vector.tensor_tensor(T.out[:], T.acc[:], ap, AluOpType.max).then_inc(S.vout, 1)
        else:
            g.vector.tensor_tensor(T.acc[:], T.acc[:], ap, AluOpType.max).then_inc(S.vacc, 1)

    if steps:
        g.sync.wait_ge(S.vout, 1)
        g.sync.dma_start(T.y[:], T.out[:]).then_inc(S.st, 16)
    else:
        g.sync.wait_ge(S.vp, 1)
        g.sync.dma_start(T.y[:], block(me)).then_inc(S.st, 16)
    g.sync.wait_ge(S.st, 16)
